import numpy as np
import ml_dtypes


def mxq(x, axis, fmt="e4m3"):
    dtype, down = {"e4m3": (ml_dtypes.float8_e4m3fn, 7), "e5m2": (ml_dtypes.float8_e5m2, 14)}[fmt]
    v = np.moveaxis(np.asarray(x, np.float32).astype(ml_dtypes.bfloat16).astype(np.float64), axis, -1)
    blocks = v.reshape(v.shape[:-1] + (-1, 32))
    amax = np.abs(blocks).max(-1, keepdims=True)
    byte = np.maximum(np.where(amax > 0, np.frexp(amax)[1] - 1 + 127, 0) - down, 1)
    scale = np.exp2(byte - 127.0)
    codes = (blocks / scale).astype(np.float32).astype(dtype).astype(np.float64)
    return np.moveaxis((codes * scale).reshape(v.shape), -1, axis)


WIDE = False


def mx_kscale(k):
    if not WIDE:
        return np.ones(k)
    levels = np.array([10, -10, 5, -5, 0])
    if k % 512:
        return np.exp2(np.random.permutation(np.resize(levels, k // 32))).repeat(32)
    a = np.empty((k // 512, 16))
    for p in range(k // 512):
        a[p, :8] = np.random.permutation(np.resize(levels, 8))
        for g in range(8):
            far = levels[np.abs(levels - a[p, g]) >= 10]
            a[p, g + 8] = far[np.random.randint(len(far))]
    return np.exp2(a.ravel()).repeat(32)


def f64(x):
    return np.asarray(x).astype(np.float64)


def striped(idx):
    return np.tile(idx.reshape(-1, 16).T, (8, 1)).astype(np.uint16)


def unstriped(offs):
    return offs[:16].T.reshape(-1).astype(np.int64)


def pack_weight(w):
    k, n = w.shape
    w = f64(np.asarray(w, np.float32).astype(ml_dtypes.bfloat16)).reshape(k // 32, 32, n)
    amax = np.abs(w).max(1)
    byte = np.clip(np.where(amax > 0, np.frexp(amax)[1] - 1 + 127 - 7, 1), 1, 254)
    scaled = (w * np.exp2(127.0 - byte)[:, None, :]).reshape(k, n).astype(np.float32)
    words = np.ascontiguousarray(scaled.reshape(k // 512, 128, 4, n).transpose(0, 1, 3, 2)).astype(ml_dtypes.float8_e4m3fn).view(np.uint8)
    return words, np.ascontiguousarray(byte.astype(np.uint8).reshape(k // 512, 16, n))


def unpack_weight(words, scales):
    g, p, n, _ = words.shape
    vals = np.ascontiguousarray(words).view(ml_dtypes.float8_e4m3fn).astype(np.float64) * np.repeat(np.exp2(scales.astype(np.float64) - 127.0), 8, axis=1)[..., None]
    return vals.transpose(0, 1, 3, 2).reshape(g * 512, n)


def sigmoid(v):
    return 1.0 / (1.0 + np.exp(-np.maximum(v, -700.0)))


K, T, S, N, U = 512, 1024, 256, 128, 512
P = 2 ** 7


def setup_inputs():
    n = np.random.standard_normal
    s = mx_kscale(K)[:, None]
    packed_xT = pack_weight(n((K, T)) * s)
    return {
        "x_words": packed_xT[0],
        "x_scales": packed_xT[1],
        "w1": (n((K, N)) / np.sqrt(K) / s).astype(np.float32),
        "w2": (n((K, N)) / np.sqrt(K) / s).astype(np.float32),
        "w3": (n((K, N)) / np.sqrt(K) / s).astype(np.float32),
        "w4": (n((K, N)) / np.sqrt(K) / s).astype(np.float32),
        "logm": (np.tile(n(U) * 0.8, (P, 1))).astype(np.float32),
        "one": (np.random.uniform(0.7, 1.3, (N, 1))).astype(np.float32),
        "sig2": (np.tile(np.random.uniform(0.05, 0.4, U), (P, 1))).astype(np.float32),
        "mat": (np.tile(np.random.uniform(0.3, 2.0, U), (P, 1))).astype(np.float32),
        "offs": striped(np.random.permutation(T)[:S]),
        "slc": striped(np.random.permutation(np.concatenate([np.arange(S), np.random.randint(0, S, U - S)]))),
    }


def reference(x_words, x_scales, w1, w2, w3, w4, logm, one, sig2, mat, offs, slc):
    xq = unpack_weight(x_words, x_scales)[:, unstriped(offs)]
    ya = mxq(f64(w1), 0, "e4m3").T @ xq
    lev = np.log(np.exp(ya) + 1.0) + 0.2
    lg = lev[:, unstriped(slc)]
    yb = mxq(f64(w2), 0, "e4m3").T @ xq
    ang = 0.6 * sigmoid(yb)
    ag = ang[:, unstriped(slc)]
    yr = mxq(f64(w3), 0, "e4m3").T @ xq
    rho = 0.8 * np.tanh(yr)
    rg = rho[:, unstriped(slc)]
    ym = mxq(f64(w4), 0, "e4m3").T @ xq
    ctr = 0.3 * ym
    cg = ctr[:, unstriped(slc)]
    dk = f64(logm)[:1] - cg
    rt = np.sqrt(f64(one) * ((dk) ** 2) + f64(sig2)[:1])
    wv = lg + ag * (rg * dk + rt)
    return np.sqrt(wv / f64(mat)[:1])

@@ -1,0 +1,159 @@
+from contextlib import ExitStack
+
+import concourse.mybir as mybir
+from concourse.masks import make_identity
+
+K, T, S, N, U = 512, 1024, 256, 128, 512
+FLOPS = 4 * 2 * K * N * S
+
+F32 = mybir.dt.float32
+BF16 = mybir.dt.bfloat16
+I32 = mybir.dt.int32
+U32 = mybir.dt.uint32
+U16 = mybir.dt.uint16
+U8 = mybir.dt.uint8
+FP8X4 = mybir.dt.float8_e4m3fn_x4
+ACT = mybir.ActivationFunctionType
+ALU = mybir.AluOpType
+
+P = 128
+PACK = 4
+SPARE = 16
+HALF = U // 2
+TINY = 2.0**-63
+
+
+def tile_picked_ysviw_vol_p_kernel(
+    tc, x_words, x_scales, w1, w2, w3, w4, logm, one, sig2, mat, offs, slc, out
+):
+    nc = tc.nc
+    with ExitStack() as ctx:
+        keep = ctx.enter_context(tc.tile_pool(name="keep", bufs=1))
+        psum = ctx.enter_context(tc.psum_pool(name="psum", bufs=1))
+
+        def sb(name, shape, dtype):
+            return keep.tile(shape, dtype, name=name, align_bytes=64)
+
+        offs_sb = keep.tile([P, S // 16], U16, name="offs_sb")
+        slc_sb = keep.tile([P, U // 16], U16, name="slc_sb")
+
+        x_all = sb("x_all", [P, T], I32)
+        xs_all = sb("xs_all", [P, T], U8)
+        nc.vector.memset(xs_all[:].bitcast(I32), 0)
+        nc.sync.dma_start(offs_sb[:], offs)
+        nc.sync.dma_start(slc_sb[:], slc)
+        nc.sync.dma_start(out=x_all[:], in_=x_words[0].rearrange("p n t -> p (n t)").bitcast(I32))
+        for r in range(4):
+            nc.sync.dma_start(
+                out=xs_all[:].bitcast(I32)[r:P:32, :], in_=x_scales[0].bitcast(I32)[r:16:4, :]
+            )
+
+        names = ("ctr", "ang", "rho", "lev")
+        weights = dict(zip(names, (w4, w2, w3, w1)))
+        raw = {}
+        for name in names:
+            raw[name] = sb("raw_" + name, [P, PACK, N], F32)
+            nc.sync.dma_start(out=raw[name][:], in_=weights[name].rearrange("(p j) n -> p j n", j=PACK))
+        logm_sb = sb("logm_sb", [P, U], F32)
+        nc.sync.dma_start(out=logm_sb[:], in_=logm)
+        one_sb = sb("one_sb", [P, 1], F32)
+        nc.sync.dma_start(out=one_sb[:], in_=one)
+        sig2_sb = sb("sig2_sb", [P, U], F32)
+        nc.sync.dma_start(out=sig2_sb[:], in_=sig2)
+        mat4 = sb("mat4", [P, 4], F32)
+        nc.sync.dma_start(out=mat4[:], in_=mat[0].rearrange("(p t) -> p t", t=4))
+
+        window = {}
+        for name in ("ctr", "ang", "tilt", "lev"):
+            window[name] = sb("window_" + name, [P, S + SPARE], F32)
+        for name in ("ctr", "tilt", "lev"):
+            nc.gpsimd.memset(window[name][:, S:], 0.0)
+        nc.scalar.activation(window["ang"][:, S:], window["ctr"][:, S:], ACT.Sigmoid)
+        tiny = sb("tiny", [P, 1], F32)
+        nc.gpsimd.memset(tiny[:], TINY)
+        ident = sb("ident", [P, P], F32)
+        make_identity(nc, ident[:])
+
+        xs = sb("xs", [P, S], U8)
+        nc.vector.tensor_copy(xs[:], xs_all[:].indirect(offs_sb[:]))
+        xw = sb("xw", [P, S], U32)
+        nc.vector.tensor_copy(xw[:], x_all[:].bitcast(U32).indirect(offs_sb[:]))
+
+        y = {}
+        for name in names:
+            grouped = sb("grouped_" + name, [P, N, PACK], BF16)
+            cast = nc.scalar.copy if name in ("ctr", "ang") else nc.vector.tensor_copy
+            cast(out=grouped[:], in_=raw[name][:].rearrange("p j n -> p n j"))
+            codes = sb("codes_" + name, [P, N], U32)
+            scales = sb("scales_" + name, [P, N], U8)
+            nc.vector.quantize_mx(
+                out=codes[:].bitcast(FP8X4), scales=scales[:], in_=grouped[:].rearrange("p n j -> p (n j)")
+            )
+            y[name] = psum.tile([P, S], F32, name="y_" + name)
+            nc.tensor.matmul_mx(
+                out=y[name][:],
+                lhsT=codes[:].bitcast(FP8X4),
+                lhsT_scale=scales[:],
+                rhs=xw[:].bitcast(FP8X4),
+                rhs_scale=xs[:],
+                start=True,
+                stop=True,
+            )
+
+        inv4 = sb("inv4", [P, 4], F32)
+        nc.vector.reciprocal(inv4[:], mat4[:])
+        inv_mat = psum.tile([P, 4, P], F32, name="inv_mat")
+        for t in range(4):
+            nc.tensor.transpose(inv_mat[:, t, :], inv4[:, t : t + 1].to_broadcast([P, P]), ident[:])
+
+        root = sb("root", [P, U], F32)
+        sig_neg = root[:, HALF // 2 : HALF // 2 + S]
+        rho = sb("rho", [P, S], F32)
+        log_sig = sb("log_sig", [P, S], F32)
+        nc.scalar.activation(window["ctr"][:, :S], y["ctr"][:], ACT.Copy, scale=-0.3)
+        nc.scalar.activation(window["ang"][:, :S], y["ang"][:], ACT.Sigmoid)
+        nc.scalar.activation(rho[:], y["rho"][:], ACT.Tanh)
+        nc.scalar.activation(sig_neg, y["lev"][:], ACT.Sigmoid, scale=-1.0)
+        nc.scalar.activation(log_sig[:], sig_neg, ACT.Ln, bias=tiny[:])
+
+        halves = [
+            (h, slice(h * HALF, (h + 1) * HALF), slc_sb[:, h * HALF // 16 : (h + 1) * HALF // 16]) for h in range(2)
+        ]
+
+        dk = sb("dk", [P, U], F32)
+        sq = sb("sq", [P, U], F32)
+        q = sb("q", [P, U], F32)
+        slope = sb("slope", [P, U], F32)
+        base = sb("base", [P, U], F32)
+        curve = sb("curve", [P, U], F32)
+        res = sb("res", [P, U], F32)
+        for h, c, idx in halves:
+            nc.vector.tensor_tensor(dk[:, c], window["ctr"][:].indirect(idx), logm_sb[:, c], ALU.add)
+            nc.scalar.activation(sq[:, c], dk[:, c], ACT.Square)
+        nc.vector.scalar_tensor_tensor(
+            window["tilt"][:, :S], window["ang"][:, :S], 0.48, rho[:], ALU.mult, ALU.mult
+        )
+        for h, c, idx in halves:
+            nc.vector.scalar_tensor_tensor(q[:, c], sq[:, c], one_sb[:], sig2_sb[:, c], ALU.mult, ALU.add)
+            nc.scalar.activation(root[:, c], q[:, c], ACT.Sqrt, scale=0.36)
+        for h, c, idx in halves:
+            nc.vector.tensor_tensor(slope[:, c], window["tilt"][:].indirect(idx), dk[:, c], ALU.mult)
+        nc.vector.scalar_tensor_tensor(
+            window["lev"][:, :S], log_sig[:], -1.0, y["lev"][:], ALU.mult, ALU.max
+        )
+        for h, c, idx in halves:
+            nc.vector.tensor_tensor(base[:, c], window["lev"][:].indirect(idx), slope[:, c], ALU.add)
+        for h, c, idx in halves:
+            nc.vector.tensor_tensor(curve[:, c], window["ang"][:].indirect(idx), root[:, c], ALU.mult)
+        for h, c, idx in halves:
+            nc.vector.scalar_tensor_tensor(sq[:, c], curve[:, c], 0.2, base[:, c], ALU.add, ALU.add)
+        for h, c, idx in halves:
+            rows = slice(h * HALF // 4, (h + 1) * HALF // 4)
+            nc.vector.tensor_tensor(
+                q[:, c].rearrange("p (a t) -> p a t", t=4),
+                sq[:, c].rearrange("p (a t) -> p a t", t=4),
+                inv_mat[:, :, rows].rearrange("p t a -> p a t"),
+                ALU.mult,
+            )
+            nc.scalar.activation(res[:, c], q[:, c], ACT.Sqrt)
+            nc.sync.dma_start(out=out[:, c], in_=res[:, c])

@@ -1,7 +1,6 @@
 from contextlib import ExitStack
 
 import concourse.mybir as mybir
-from concourse.masks import make_identity
 
 K, T, S, N, U = 512, 1024, 256, 128, 512
 FLOPS = 4 * 2 * K * N * S
@@ -18,9 +17,10 @@ ALU = mybir.AluOpType
 
 P = 128
 PACK = 4
+QUAD = 32
 SPARE = 16
 HALF = U // 2
-TINY = 2.0**-63
+TINY_ROOT = 2.0**-31
 
 
 def tile_picked_ysviw_vol_p_kernel(
@@ -40,119 +40,146 @@ def tile_picked_ysviw_vol_p_kernel(
         x_all = sb("x_all", [P, T], I32)
         xs_all = sb("xs_all", [P, T], U8)
         nc.vector.memset(xs_all[:].bitcast(I32), 0)
-        nc.sync.dma_start(offs_sb[:], offs)
-        nc.sync.dma_start(slc_sb[:], slc)
-        nc.sync.dma_start(out=x_all[:], in_=x_words[0].rearrange("p n t -> p (n t)").bitcast(I32))
-        for r in range(4):
-            nc.sync.dma_start(
-                out=xs_all[:].bitcast(I32)[r:P:32, :], in_=x_scales[0].bitcast(I32)[r:16:4, :]
-            )
 
         names = ("ctr", "ang", "rho", "lev")
         weights = dict(zip(names, (w4, w2, w3, w1)))
-        raw = {}
-        for name in names:
-            raw[name] = sb("raw_" + name, [P, PACK, N], F32)
-            nc.sync.dma_start(out=raw[name][:], in_=weights[name].rearrange("(p j) n -> p j n", j=PACK))
-        logm_sb = sb("logm_sb", [P, U], F32)
-        nc.sync.dma_start(out=logm_sb[:], in_=logm)
-        one_sb = sb("one_sb", [P, 1], F32)
-        nc.sync.dma_start(out=one_sb[:], in_=one)
-        sig2_sb = sb("sig2_sb", [P, U], F32)
-        nc.sync.dma_start(out=sig2_sb[:], in_=sig2)
-        mat4 = sb("mat4", [P, 4], F32)
-        nc.sync.dma_start(out=mat4[:], in_=mat[0].rearrange("(p t) -> p t", t=4))
+        raw = {name: sb("raw_" + name, [P, PACK * N], F32) for name in names}
+
+        def load_weight(name):
+            nc.sync.dma_start(out=raw[name][:], in_=weights[name].rearrange("(p j) n -> p (j n)", j=PACK))
 
         window = {}
-        for name in ("ctr", "ang", "tilt", "lev"):
-            window[name] = sb("window_" + name, [P, S + SPARE], F32)
-        for name in ("ctr", "tilt", "lev"):
-            nc.gpsimd.memset(window[name][:, S:], 0.0)
-        nc.scalar.activation(window["ang"][:, S:], window["ctr"][:, S:], ACT.Sigmoid)
-        tiny = sb("tiny", [P, 1], F32)
-        nc.gpsimd.memset(tiny[:], TINY)
-        ident = sb("ident", [P, P], F32)
-        make_identity(nc, ident[:])
-
-        xs = sb("xs", [P, S], U8)
-        nc.vector.tensor_copy(xs[:], xs_all[:].indirect(offs_sb[:]))
-        xw = sb("xw", [P, S], U32)
-        nc.vector.tensor_copy(xw[:], x_all[:].bitcast(U32).indirect(offs_sb[:]))
-
-        y = {}
+        for name, width in (("ctr", U + SPARE), ("ang", U + SPARE), ("tilt", S + U + 1), ("lev", HALF + SPARE)):
+            window[name] = sb("window_" + name, [P, width], F32)
+        logm_sb = window["tilt"][:, :U]
+        sq = window["tilt"][:, S:]
+        log_sig = window["ang"][:, S:U]
+        one_sb = sb("one_sb", [P, 1], F32)
+        sig2_sb = sb("sig2_sb", [P, U], F32)
+        mat4 = sb("mat4", [P, 4], F32)
+        nc.sync.dma_start(offs_sb[:], offs)
+        nc.scalar.dma_start(out=mat4[:], in_=mat[0].rearrange("(p t) -> p t", t=4))
+        nc.sync.dma_start(out=x_all[:], in_=x_words[0].rearrange("p n t -> p (n t)").bitcast(I32))
+        for r in range(4):
+            nc.sync.dma_start(out=xs_all[:].bitcast(I32)[r:P:QUAD, :], in_=x_scales[0].bitcast(I32)[r:16:4, :])
         for name in names:
-            grouped = sb("grouped_" + name, [P, N, PACK], BF16)
-            cast = nc.scalar.copy if name in ("ctr", "ang") else nc.vector.tensor_copy
-            cast(out=grouped[:], in_=raw[name][:].rearrange("p j n -> p n j"))
-            codes = sb("codes_" + name, [P, N], U32)
-            scales = sb("scales_" + name, [P, N], U8)
-            nc.vector.quantize_mx(
-                out=codes[:].bitcast(FP8X4), scales=scales[:], in_=grouped[:].rearrange("p n j -> p (n j)")
-            )
-            y[name] = psum.tile([P, S], F32, name="y_" + name)
-            nc.tensor.matmul_mx(
-                out=y[name][:],
-                lhsT=codes[:].bitcast(FP8X4),
-                lhsT_scale=scales[:],
-                rhs=xw[:].bitcast(FP8X4),
-                rhs_scale=xs[:],
-                start=True,
-                stop=True,
-            )
+            load_weight(name)
+        nc.sync.dma_start(slc_sb[:], slc)
+        nc.sync.dma_start(out=logm_sb, in_=logm)
+        nc.sync.dma_start(out=sig2_sb[:], in_=sig2)
+        nc.sync.dma_start(out=one_sb[:], in_=one)
+
+        stage = sb("stage", [P, 4 * N * PACK], BF16)
+        staged = {name: stage[:, i * N * PACK : (i + 1) * N * PACK] for i, name in enumerate(names)}
+        dk_and_guard = sb("dk_and_guard", [P, U + 1], F32)
+        dk, guard = dk_and_guard[:, :U], dk_and_guard[:, U:]
+        nc.vector.memset(guard, TINY_ROOT)
+        warm = sb("warm", [P, 1], F32)
+        nc.scalar.activation(warm[:], guard, ACT.Sigmoid)
+
+        ones = sb("ones", [P, QUAD], F32)
+        column = sb("column", [P, QUAD], F32)
+        row = sb("row", [P, QUAD], F32)
+        ident = sb("ident", [P, P], F32)
+        nc.vector.memset(ones[:], 1.0)
+        nc.vector.memset(ident[:], 0.0)
+        nc.vector.tensor_tensor_scan(column[:], ones[:], ones[:], 0.0, ALU.mult, ALU.add)
+        nc.vector.transpose(row[:], column[:])
+        for a in range(0, P, QUAD):
+            quad = slice(a, a + QUAD)
+            nc.vector.tensor_tensor(ident[quad, quad], column[quad, :], row[quad, :], ALU.is_equal)
+        for name, written in (("ctr", S), ("ang", U), ("lev", S)):
+            nc.vector.memset(window[name][:, written:], 0.0)
 
         inv4 = sb("inv4", [P, 4], F32)
         nc.vector.reciprocal(inv4[:], mat4[:])
-        inv_mat = psum.tile([P, 4, P], F32, name="inv_mat")
+        inv_bank = psum.tile([P, 4, P], F32, name="inv_bank")
         for t in range(4):
-            nc.tensor.transpose(inv_mat[:, t, :], inv4[:, t : t + 1].to_broadcast([P, P]), ident[:])
+            nc.tensor.transpose(inv_bank[:, t, :], inv4[:, t : t + 1].to_broadcast([P, P]), ident[:])
+        inv_mat = inv_bank[:].rearrange("p t a -> p a t")
+
+        def interleave(name, copy):
+            copy(
+                out=staged[name].rearrange("p (n j) -> p n j", j=PACK),
+                in_=raw[name][:].rearrange("p (j n) -> p n j", j=PACK),
+            )
+
+        xw = sb("xw", [P, S], U32)
+        nc.vector.tensor_copy(xw[:], x_all[:].bitcast(U32).indirect(offs_sb[:]))
+        xs = sb("xs", [P, S], U8)
+        nc.vector.tensor_copy(xs[:], xs_all[:].indirect(offs_sb[:]))
+
+        y = {}
+
+        def products(*group):
+            first = names.index(group[0])
+            codes = sb("codes_" + group[0], [P, len(group) * N], U32)
+            scales = sb("scales_" + group[0], [P, len(group) * N], U8)
+            nc.vector.quantize_mx(
+                out=codes[:].bitcast(FP8X4),
+                scales=scales[:],
+                in_=stage[:, first * N * PACK : (first + len(group)) * N * PACK],
+            )
+            for i, name in enumerate(group):
+                y[name] = psum.tile([P, S], F32, name="y_" + name)
+                nc.tensor.matmul_mx(
+                    out=y[name][:],
+                    lhsT=codes[:, i * N : (i + 1) * N].bitcast(FP8X4),
+                    lhsT_scale=scales[:, i * N : (i + 1) * N],
+                    rhs=xw[:].bitcast(FP8X4),
+                    rhs_scale=xs[:],
+                    start=True,
+                    stop=True,
+                )
+
+        interleave("ctr", nc.scalar.copy)
+        products("ctr")
+        interleave("ang", nc.scalar.copy)
+        nc.scalar.activation(window["ctr"][:, :S], y["ctr"][:], ACT.Copy, scale=-0.3)
+        interleave("rho", nc.vector.tensor_copy)
+        products("ang")
+        interleave("lev", nc.vector.tensor_copy)
+        products("rho", "lev")
 
         root = sb("root", [P, U], F32)
-        sig_neg = root[:, HALF // 2 : HALF // 2 + S]
-        rho = sb("rho", [P, S], F32)
-        log_sig = sb("log_sig", [P, S], F32)
-        nc.scalar.activation(window["ctr"][:, :S], y["ctr"][:], ACT.Copy, scale=-0.3)
-        nc.scalar.activation(window["ang"][:, :S], y["ang"][:], ACT.Sigmoid)
-        nc.scalar.activation(rho[:], y["rho"][:], ACT.Tanh)
+        sig_neg = root[:, :S]
+        sig_b = sb("sig_b", [P, S], F32)[:]
+        rho = sb("rho", [P, S], F32)[:]
+        nc.scalar.activation(sig_b, y["ang"][:], ACT.Sigmoid)
+        nc.scalar.activation(rho, y["rho"][:], ACT.Tanh)
+        nc.scalar.activation(window["ang"][:, :S], sig_b, ACT.Square, scale=0.6)
         nc.scalar.activation(sig_neg, y["lev"][:], ACT.Sigmoid, scale=-1.0)
-        nc.scalar.activation(log_sig[:], sig_neg, ACT.Ln, bias=tiny[:])
 
-        halves = [
-            (h, slice(h * HALF, (h + 1) * HALF), slc_sb[:, h * HALF // 16 : (h + 1) * HALF // 16]) for h in range(2)
-        ]
+        def pieces(*edges):
+            return [(slice(a, b), slc_sb[:, a // 16 : b // 16]) for a, b in zip(edges, edges[1:])]
 
-        dk = sb("dk", [P, U], F32)
-        sq = sb("sq", [P, U], F32)
+        total = sb("total", [P, U], F32)
         q = sb("q", [P, U], F32)
         slope = sb("slope", [P, U], F32)
         base = sb("base", [P, U], F32)
         curve = sb("curve", [P, U], F32)
         res = sb("res", [P, U], F32)
-        for h, c, idx in halves:
-            nc.vector.tensor_tensor(dk[:, c], window["ctr"][:].indirect(idx), logm_sb[:, c], ALU.add)
-            nc.scalar.activation(sq[:, c], dk[:, c], ACT.Square)
-        nc.vector.scalar_tensor_tensor(
-            window["tilt"][:, :S], window["ang"][:, :S], 0.48, rho[:], ALU.mult, ALU.mult
-        )
-        for h, c, idx in halves:
-            nc.vector.scalar_tensor_tensor(q[:, c], sq[:, c], one_sb[:], sig2_sb[:, c], ALU.mult, ALU.add)
-            nc.scalar.activation(root[:, c], q[:, c], ACT.Sqrt, scale=0.36)
-        for h, c, idx in halves:
-            nc.vector.tensor_tensor(slope[:, c], window["tilt"][:].indirect(idx), dk[:, c], ALU.mult)
-        nc.vector.scalar_tensor_tensor(
-            window["lev"][:, :S], log_sig[:], -1.0, y["lev"][:], ALU.mult, ALU.max
-        )
-        for h, c, idx in halves:
+        nc.vector.tensor_tensor(dk, window["ctr"][:].indirect(slc_sb[:]), logm_sb, ALU.add)
+        nc.scalar.activation(sq, dk_and_guard[:], ACT.Square)
+        nc.scalar.activation(log_sig, sig_neg, ACT.Ln, bias=sq[:, U:])
+        nc.scalar.activation(warm[:], log_sig[:, 0:1], ACT.Sqrt, bias=sq[:, U:], scale=0.0)
+        nc.vector.scalar_tensor_tensor(window["tilt"][:, :S], sig_b, 0.48, rho, ALU.mult, ALU.mult)
+        nc.vector.scalar_tensor_tensor(q[:], sq[:, :U], one_sb[:], sig2_sb[:], ALU.mult, ALU.add)
+        nc.vector.tensor_tensor(slope[:], window["tilt"][:].indirect(slc_sb[:]), dk, ALU.mult)
+        nc.vector.scalar_tensor_tensor(window["lev"][:, :S], log_sig, -1.0, y["lev"][:], ALU.mult, ALU.max)
+        nc.vector.tensor_tensor(curve[:], window["ang"][:].indirect(slc_sb[:]), q[:], ALU.mult)
+        nc.scalar.activation(root[:], curve[:], ACT.Sqrt)
+
+        tail = pieces(0, HALF, U)
+        for c, idx in tail:
             nc.vector.tensor_tensor(base[:, c], window["lev"][:].indirect(idx), slope[:, c], ALU.add)
-        for h, c, idx in halves:
-            nc.vector.tensor_tensor(curve[:, c], window["ang"][:].indirect(idx), root[:, c], ALU.mult)
-        for h, c, idx in halves:
-            nc.vector.scalar_tensor_tensor(sq[:, c], curve[:, c], 0.2, base[:, c], ALU.add, ALU.add)
-        for h, c, idx in halves:
-            rows = slice(h * HALF // 4, (h + 1) * HALF // 4)
+        for c, idx in tail:
+            nc.vector.scalar_tensor_tensor(total[:, c], root[:, c], 0.2, base[:, c], ALU.add, ALU.add)
+        for c, idx in tail:
             nc.vector.tensor_tensor(
                 q[:, c].rearrange("p (a t) -> p a t", t=4),
-                sq[:, c].rearrange("p (a t) -> p a t", t=4),
-                inv_mat[:, :, rows].rearrange("p t a -> p a t"),
+                total[:, c].rearrange("p (a t) -> p a t", t=4),
+                inv_mat[:, c.start // 4 : c.stop // 4, :],
                 ALU.mult,
             )
             nc.scalar.activation(res[:, c], q[:, c], ACT.Sqrt)

@@ -49,11 +49,9 @@ def tile_picked_ysviw_vol_p_kernel(
             nc.sync.dma_start(out=raw[name][:], in_=weights[name].rearrange("(p j) n -> p (j n)", j=PACK))
 
         window = {}
-        for name, width in (("ctr", U + SPARE), ("ang", U + SPARE), ("tilt", S + U + 1), ("lev", HALF + SPARE)):
+        for name, width in (("ctr", S + SPARE), ("ang", S + SPARE), ("tilt", U), ("lev", S + SPARE)):
             window[name] = sb("window_" + name, [P, width], F32)
-        logm_sb = window["tilt"][:, :U]
-        sq = window["tilt"][:, S:]
-        log_sig = window["ang"][:, S:U]
+        logm_sb = window["tilt"]
         one_sb = sb("one_sb", [P, 1], F32)
         sig2_sb = sb("sig2_sb", [P, U], F32)
         mat4 = sb("mat4", [P, 4], F32)
@@ -65,9 +63,9 @@ def tile_picked_ysviw_vol_p_kernel(
         for name in names:
             load_weight(name)
         nc.sync.dma_start(slc_sb[:], slc)
-        nc.sync.dma_start(out=logm_sb, in_=logm)
+        nc.sync.dma_start(out=logm_sb[:], in_=logm)
         nc.sync.dma_start(out=sig2_sb[:], in_=sig2)
-        nc.sync.dma_start(out=one_sb[:], in_=one)
+        nc.gpsimd.dma_start(out=one_sb[:], in_=one)
 
         stage = sb("stage", [P, 4 * N * PACK], BF16)
         staged = {name: stage[:, i * N * PACK : (i + 1) * N * PACK] for i, name in enumerate(names)}
@@ -88,8 +86,8 @@ def tile_picked_ysviw_vol_p_kernel(
         for a in range(0, P, QUAD):
             quad = slice(a, a + QUAD)
             nc.vector.tensor_tensor(ident[quad, quad], column[quad, :], row[quad, :], ALU.is_equal)
-        for name, written in (("ctr", S), ("ang", U), ("lev", S)):
-            nc.vector.memset(window[name][:, written:], 0.0)
+        for name in ("ctr", "ang", "lev"):
+            nc.vector.memset(window[name][:, S:], 0.0)
 
         inv4 = sb("inv4", [P, 4], F32)
         nc.vector.reciprocal(inv4[:], mat4[:])
@@ -137,12 +135,15 @@ def tile_picked_ysviw_vol_p_kernel(
         interleave("ang", nc.scalar.copy)
         nc.scalar.activation(window["ctr"][:, :S], y["ctr"][:], ACT.Copy, scale=-0.3)
         interleave("rho", nc.vector.tensor_copy)
-        products("ang")
+        products("ang", "rho")
         interleave("lev", nc.vector.tensor_copy)
-        products("rho", "lev")
+        products("lev")
 
         root = sb("root", [P, U], F32)
-        sig_neg = root[:, :S]
+        curve = sb("curve", [P, U], F32)
+        sig_neg = curve[:, HALF:]
+        log_sig = sb("log_sig", [P, S], F32)[:]
+        sq = sb("sq", [P, U + 1], F32)
         sig_b = sb("sig_b", [P, S], F32)[:]
         rho = sb("rho", [P, S], F32)[:]
         nc.scalar.activation(sig_b, y["ang"][:], ACT.Sigmoid)
@@ -157,20 +158,24 @@ def tile_picked_ysviw_vol_p_kernel(
         q = sb("q", [P, U], F32)
         slope = sb("slope", [P, U], F32)
         base = sb("base", [P, U], F32)
-        curve = sb("curve", [P, U], F32)
         res = sb("res", [P, U], F32)
-        nc.vector.tensor_tensor(dk, window["ctr"][:].indirect(slc_sb[:]), logm_sb, ALU.add)
-        nc.scalar.activation(sq, dk_and_guard[:], ACT.Square)
+        tail = pieces(0, HALF, U)
+        (first, first_idx), (second, second_idx) = tail
+        for c, idx in tail:
+            nc.vector.tensor_tensor(dk[:, c], window["ctr"][:].indirect(idx), logm_sb[:, c], ALU.add)
+        nc.scalar.activation(sq[:, :HALF], dk_and_guard[:, :HALF], ACT.Square)
+        nc.scalar.activation(sq[:, HALF:], dk_and_guard[:, HALF:], ACT.Square)
         nc.scalar.activation(log_sig, sig_neg, ACT.Ln, bias=sq[:, U:])
         nc.scalar.activation(warm[:], log_sig[:, 0:1], ACT.Sqrt, bias=sq[:, U:], scale=0.0)
         nc.vector.scalar_tensor_tensor(window["tilt"][:, :S], sig_b, 0.48, rho, ALU.mult, ALU.mult)
-        nc.vector.scalar_tensor_tensor(q[:], sq[:, :U], one_sb[:], sig2_sb[:], ALU.mult, ALU.add)
-        nc.vector.tensor_tensor(slope[:], window["tilt"][:].indirect(slc_sb[:]), dk, ALU.mult)
+        for c, idx in tail:
+            nc.vector.scalar_tensor_tensor(q[:, c], sq[:, c], one_sb[:], sig2_sb[:, c], ALU.mult, ALU.add)
+            nc.vector.tensor_tensor(slope[:, c], window["tilt"][:].indirect(idx), dk[:, c], ALU.mult)
+        nc.vector.tensor_tensor(curve[:, first], window["ang"][:].indirect(first_idx), q[:, first], ALU.mult)
         nc.vector.scalar_tensor_tensor(window["lev"][:, :S], log_sig, -1.0, y["lev"][:], ALU.mult, ALU.max)
-        nc.vector.tensor_tensor(curve[:], window["ang"][:].indirect(slc_sb[:]), q[:], ALU.mult)
+        nc.vector.tensor_tensor(curve[:, second], window["ang"][:].indirect(second_idx), q[:, second], ALU.mult)
         nc.scalar.activation(root[:], curve[:], ACT.Sqrt)
 
-        tail = pieces(0, HALF, U)
         for c, idx in tail:
             nc.vector.tensor_tensor(base[:, c], window["lev"][:].indirect(idx), slope[:, c], ALU.add)
         for c, idx in tail:

from contextlib import ExitStack

import concourse.mybir as mybir

K, T, S, N, U = 512, 1024, 256, 128, 512
FLOPS = 4 * 2 * K * N * S

F32 = mybir.dt.float32
BF16 = mybir.dt.bfloat16
I32 = mybir.dt.int32
U32 = mybir.dt.uint32
U16 = mybir.dt.uint16
U8 = mybir.dt.uint8
FP8X4 = mybir.dt.float8_e4m3fn_x4
ACT = mybir.ActivationFunctionType
ALU = mybir.AluOpType

P = 128
PACK = 4
QUAD = 32
SPARE = 16
HALF = U // 2
TINY_ROOT = 2.0**-31


def tile_picked_ysviw_vol_p_kernel(
    tc, x_words, x_scales, w1, w2, w3, w4, logm, one, sig2, mat, offs, slc, out
):
    nc = tc.nc
    with ExitStack() as ctx:
        keep = ctx.enter_context(tc.tile_pool(name="keep", bufs=1))
        psum = ctx.enter_context(tc.psum_pool(name="psum", bufs=1))

        def sb(name, shape, dtype):
            return keep.tile(shape, dtype, name=name, align_bytes=64)

        offs_sb = keep.tile([P, S // 16], U16, name="offs_sb")
        slc_sb = keep.tile([P, U // 16], U16, name="slc_sb")

        x_all = sb("x_all", [P, T], I32)
        xs_all = sb("xs_all", [P, T], U8)
        nc.vector.memset(xs_all[:].bitcast(I32), 0)

        names = ("ctr", "ang", "rho", "lev")
        weights = dict(zip(names, (w4, w2, w3, w1)))
        raw = {name: sb("raw_" + name, [P, PACK * N], F32) for name in names}

        def load_weight(name):
            nc.sync.dma_start(out=raw[name][:], in_=weights[name].rearrange("(p j) n -> p (j n)", j=PACK))

        window = {}
        for name, width in (("ctr", S + SPARE), ("ang", S + SPARE), ("tilt", U), ("lev", S + SPARE)):
            window[name] = sb("window_" + name, [P, width], F32)
        logm_sb = window["tilt"]
        one_sb = sb("one_sb", [P, 1], F32)
        sig2_sb = sb("sig2_sb", [P, U], F32)
        mat4 = sb("mat4", [P, 4], F32)
        nc.sync.dma_start(offs_sb[:], offs)
        nc.scalar.dma_start(out=mat4[:], in_=mat[0].rearrange("(p t) -> p t", t=4))
        nc.sync.dma_start(out=x_all[:], in_=x_words[0].rearrange("p n t -> p (n t)").bitcast(I32))
        for r in range(4):
            nc.sync.dma_start(out=xs_all[:].bitcast(I32)[r:P:QUAD, :], in_=x_scales[0].bitcast(I32)[r:16:4, :])
        for name in names:
            load_weight(name)
        nc.sync.dma_start(slc_sb[:], slc)
        nc.sync.dma_start(out=logm_sb[:], in_=logm)
        nc.sync.dma_start(out=sig2_sb[:], in_=sig2)
        nc.gpsimd.dma_start(out=one_sb[:], in_=one)

        stage = sb("stage", [P, 4 * N * PACK], BF16)
        staged = {name: stage[:, i * N * PACK : (i + 1) * N * PACK] for i, name in enumerate(names)}
        dk_and_guard = sb("dk_and_guard", [P, U + 1], F32)
        dk, guard = dk_and_guard[:, :U], dk_and_guard[:, U:]
        nc.vector.memset(guard, TINY_ROOT)
        warm = sb("warm", [P, 1], F32)
        nc.scalar.activation(warm[:], guard, ACT.Sigmoid)

        ones = sb("ones", [P, QUAD], F32)
        column = sb("column", [P, QUAD], F32)
        row = sb("row", [P, QUAD], F32)
        ident = sb("ident", [P, P], F32)
        nc.vector.memset(ones[:], 1.0)
        nc.vector.memset(ident[:], 0.0)
        nc.vector.tensor_tensor_scan(column[:], ones[:], ones[:], 0.0, ALU.mult, ALU.add)
        nc.vector.transpose(row[:], column[:])
        for a in range(0, P, QUAD):
            quad = slice(a, a + QUAD)
            nc.vector.tensor_tensor(ident[quad, quad], column[quad, :], row[quad, :], ALU.is_equal)
        for name in ("ctr", "ang", "lev"):
            nc.vector.memset(window[name][:, S:], 0.0)

        inv4 = sb("inv4", [P, 4], F32)
        nc.vector.reciprocal(inv4[:], mat4[:])
        inv_bank = psum.tile([P, 4, P], F32, name="inv_bank")
        for t in range(4):
            nc.tensor.transpose(inv_bank[:, t, :], inv4[:, t : t + 1].to_broadcast([P, P]), ident[:])
        inv_mat = inv_bank[:].rearrange("p t a -> p a t")

        def interleave(name, copy):
            copy(
                out=staged[name].rearrange("p (n j) -> p n j", j=PACK),
                in_=raw[name][:].rearrange("p (j n) -> p n j", j=PACK),
            )

        xw = sb("xw", [P, S], U32)
        nc.vector.tensor_copy(xw[:], x_all[:].bitcast(U32).indirect(offs_sb[:]))
        xs = sb("xs", [P, S], U8)
        nc.vector.tensor_copy(xs[:], xs_all[:].indirect(offs_sb[:]))

        y = {}

        def products(*group):
            first = names.index(group[0])
            codes = sb("codes_" + group[0], [P, len(group) * N], U32)
            scales = sb("scales_" + group[0], [P, len(group) * N], U8)
            nc.vector.quantize_mx(
                out=codes[:].bitcast(FP8X4),
                scales=scales[:],
                in_=stage[:, first * N * PACK : (first + len(group)) * N * PACK],
            )
            for i, name in enumerate(group):
                y[name] = psum.tile([P, S], F32, name="y_" + name)
                nc.tensor.matmul_mx(
                    out=y[name][:],
                    lhsT=codes[:, i * N : (i + 1) * N].bitcast(FP8X4),
                    lhsT_scale=scales[:, i * N : (i + 1) * N],
                    rhs=xw[:].bitcast(FP8X4),
                    rhs_scale=xs[:],
                    start=True,
                    stop=True,
                )

        interleave("ctr", nc.scalar.copy)
        products("ctr")
        interleave("ang", nc.scalar.copy)
        nc.scalar.activation(window["ctr"][:, :S], y["ctr"][:], ACT.Copy, scale=-0.3)
        interleave("rho", nc.vector.tensor_copy)
        products("ang", "rho")
        interleave("lev", nc.vector.tensor_copy)
        products("lev")

        root = sb("root", [P, U], F32)
        curve = sb("curve", [P, U], F32)
        sig_neg = curve[:, HALF:]
        log_sig = sb("log_sig", [P, S], F32)[:]
        sq = sb("sq", [P, U + 1], F32)
        sig_b = sb("sig_b", [P, S], F32)[:]
        rho = sb("rho", [P, S], F32)[:]
        nc.scalar.activation(sig_b, y["ang"][:], ACT.Sigmoid)
        nc.scalar.activation(rho, y["rho"][:], ACT.Tanh)
        nc.scalar.activation(window["ang"][:, :S], sig_b, ACT.Square, scale=0.6)
        nc.scalar.activation(sig_neg, y["lev"][:], ACT.Sigmoid, scale=-1.0)

        def pieces(*edges):
            return [(slice(a, b), slc_sb[:, a // 16 : b // 16]) for a, b in zip(edges, edges[1:])]

        total = sb("total", [P, U], F32)
        q = sb("q", [P, U], F32)
        slope = sb("slope", [P, U], F32)
        base = sb("base", [P, U], F32)
        res = sb("res", [P, U], F32)
        tail = pieces(0, HALF, U)
        (first, first_idx), (second, second_idx) = tail
        for c, idx in tail:
            nc.vector.tensor_tensor(dk[:, c], window["ctr"][:].indirect(idx), logm_sb[:, c], ALU.add)
        nc.scalar.activation(sq[:, :HALF], dk_and_guard[:, :HALF], ACT.Square)
        nc.scalar.activation(sq[:, HALF:], dk_and_guard[:, HALF:], ACT.Square)
        nc.scalar.activation(log_sig, sig_neg, ACT.Ln, bias=sq[:, U:])
        nc.scalar.activation(warm[:], log_sig[:, 0:1], ACT.Sqrt, bias=sq[:, U:], scale=0.0)
        nc.vector.scalar_tensor_tensor(window["tilt"][:, :S], sig_b, 0.48, rho, ALU.mult, ALU.mult)
        for c, idx in tail:
            nc.vector.scalar_tensor_tensor(q[:, c], sq[:, c], one_sb[:], sig2_sb[:, c], ALU.mult, ALU.add)
            nc.vector.tensor_tensor(slope[:, c], window["tilt"][:].indirect(idx), dk[:, c], ALU.mult)
        nc.vector.tensor_tensor(curve[:, first], window["ang"][:].indirect(first_idx), q[:, first], ALU.mult)
        nc.vector.scalar_tensor_tensor(window["lev"][:, :S], log_sig, -1.0, y["lev"][:], ALU.mult, ALU.max)
        nc.vector.tensor_tensor(curve[:, second], window["ang"][:].indirect(second_idx), q[:, second], ALU.mult)
        nc.scalar.activation(root[:], curve[:], ACT.Sqrt)

        for c, idx in tail:
            nc.vector.tensor_tensor(base[:, c], window["lev"][:].indirect(idx), slope[:, c], ALU.add)
        for c, idx in tail:
            nc.vector.scalar_tensor_tensor(total[:, c], root[:, c], 0.2, base[:, c], ALU.add, ALU.add)
        for c, idx in tail:
            nc.vector.tensor_tensor(
                q[:, c].rearrange("p (a t) -> p a t", t=4),
                total[:, c].rearrange("p (a t) -> p a t", t=4),
                inv_mat[:, c.start // 4 : c.stop // 4, :],
                ALU.mult,
            )
            nc.scalar.activation(res[:, c], q[:, c], ACT.Sqrt)
            nc.sync.dma_start(out=out[:, c], in_=res[:, c])
